import numpy as np, ml_dtypes
CORES = [51,54,179,182]
N = 4
import mx_ref
NC = 128
BF = ml_dtypes.bfloat16
def setup_inputs(rng):
    def f(*shape):
        return mx_ref.flush((rng.standard_normal(shape, dtype=np.float32) * np.exp2(rng.integers(-2, 3, shape[:-1] + (1,)))).astype(BF))
    return {"w": f(N, 128, N * 512), "x": f(N, 128, N * 4 * NC)}
def setup_inputs_blocks(rng):
    d = setup_inputs(rng)
    for k in ("w", "x"): d[k] = mx_ref.spread(d[k], rng, 1)
    return d
def setup_inputs_wide(rng):
    d = setup_inputs(rng)
    for k in ("w", "x"): d[k] = mx_ref.flush((d[k].astype(np.float32) * np.exp2(rng.integers(-8, 9, (N, 1, 1))).astype(np.float32)).astype(BF))
    return d
def setup_inputs_zeros(rng):
    d = setup_inputs(rng); v = d["x"].reshape(N, 128, -1, 4).copy()
    v[np.broadcast_to((rng.random((N, 1, v.shape[2], 1)) < 0.33), v.shape)] = 0
    d["x"] = v.reshape(d["x"].shape)
    return d
def reference(w, x):
    y = np.zeros((N, 128, NC), np.float32)
    for r in range(N):
        for j in range(N):
            p = mx_ref.matmul(mx_ref.quantize(w[r][:, 512 * j:512 * j + 512]), mx_ref.quantize(x[j][:, 4 * NC * r:4 * NC * r + 4 * NC]))
            y[r] = p if j == 0 else y[r] + p
    return {"y": y}

@@ -1,0 +1,144 @@
+from concourse.bass import DstId, RemoteDMATransfer
+from concourse.mybir import dt
+
+N = 4
+TB = 512
+TC = 128
+
+SCRATCH = {
+    "xb": ("sbuf", [128, N * TB], "bfloat16"),
+    "wb": ("sbuf", [128, N * TB], "bfloat16"),
+    "xq": ("sbuf", [128, N * TC], "float8_e4m3fn_x4"),
+    "xs": ("sbuf", [128, N * TC], "uint8"),
+    "wq": ("sbuf", [128, N * TC], "float8_e4m3fn_x4"),
+    "ws": ("sbuf", [128, N * TC], "uint8"),
+    "rq": ("sbuf", [128, (N - 1) * TC], "float8_e4m3fn_x4"),
+    "rs": ("sbuf", [128, (N - 1) * TC], "uint8"),
+    "acc": ("psum", [128, 512], "float32"),
+    "yb": ("sbuf", [128, TC], "float32"),
+}
+SEMAPHORES = ["lxf", "lxn", "lxo", "lwn", "lwf", "qxf", "qxn", "qxo", "qwn", "qwf",
+              "sent", "mm", "cp", "st"] + ["arr%d" % k for k in range(N - 1)]
+
+
+def _one_chip(topo, a, b):
+    return topo.host(a) == topo.host(b) and topo.chip(a) == topo.chip(b)
+
+
+def _runs(ranks):
+    out = []
+    for j in sorted(ranks):
+        if out and out[-1][0] + out[-1][1] == j:
+            out[-1][1] += 1
+        else:
+            out.append([j, 1])
+    return out
+
+
+def _share(engines, parts):
+    per = 1
+    while per * 2 * parts <= len(engines):
+        per *= 2
+    return [sum(1 << e for e in engines[k * per:(k + 1) * per]) for k in range(parts)]
+
+
+def _masks(topo, cores, src):
+    far = [c for c in cores if c != src and not _one_chip(topo, c, src)]
+    near = [c for c in cores if c != src and _one_chip(topo, c, src)]
+    out, used = {}, 0
+    for group in (far, near):
+        if not group:
+            continue
+        can = topo.mask(src, group[0])
+        for c in group:
+            can &= topo.mask(src, c)
+        engines = [e for e in range(can.bit_length()) if can >> e & 1]
+        free = [e for e in engines if not used >> e & 1]
+        for c, m in zip(group, _share(free if len(free) >= len(group) else engines, len(group))):
+            out[c] = m
+            used |= m
+    return out
+
+
+def _slot(r, j):
+    return j if j < r else j - 1
+
+
+def rank_program(g, core, T, topo):
+    r = T.rank_of(core)
+    if r is None:
+        return
+    cores, S = T.cores, T.sem
+    far = [j for j in range(N) if not _one_chip(topo, cores[j], core)]
+    near = [j for j in range(N) if j != r and _one_chip(topo, cores[j], core)]
+
+    def load(q, buf, src, ranks, sem):
+        for a, n in _runs(ranks):
+            q.dma_start(buf[:, a * TB:(a + n) * TB], src[:, a * TB:(a + n) * TB]).then_inc(sem, 16)
+
+    def quant(codes, plane, buf, ranks, lsem, qsem):
+        g.vector.wait_ge(lsem, 16 * len(_runs(ranks)))
+        for a, n in _runs(ranks):
+            g.vector.quantize_mx(codes[:, a * TC:(a + n) * TC], plane[:, a * TC:(a + n) * TC],
+                                 buf[:, a * TB:(a + n) * TB]).then_inc(qsem, 1)
+
+    load(g.sync, T.xb, T.x, far, S.lxf)
+    load(g.scalar, T.xb, T.x, near, S.lxn)
+    load(g.scalar, T.xb, T.x, [r], S.lxo)
+    load(g.sync, T.wb, T.w, near + [r], S.lwn)
+    load(g.scalar, T.wb, T.w, far, S.lwf)
+
+    quant(T.xq, T.xs, T.xb, far, S.lxf, S.qxf)
+    quant(T.xq, T.xs, T.xb, near, S.lxn, S.qxn)
+    quant(T.xq, T.xs, T.xb, [r], S.lxo, S.qxo)
+    quant(T.wq, T.ws, T.wb, near + [r], S.lwn, S.qwn)
+    quant(T.wq, T.ws, T.wb, far, S.lwf, S.qwf)
+
+    mine = _masks(topo, cores, core)
+    left = 0
+    for group, qsem in ((far, S.qxf), (near, S.qxn)):
+        if not group:
+            continue
+        g.wait_ge(qsem, len(_runs(group)))
+        for what in ("codes", "plane"):
+            trs = []
+            for j in group:
+                rid, pid = topo.addr(cores[j], core)
+                k = _slot(j, r)
+                if what == "codes":
+                    src = T.xq[:, j * TC:(j + 1) * TC].bitcast(dt.uint8)
+                    dst = T.rq[:, k * TC:(k + 1) * TC].bitcast(dt.uint8)
+                else:
+                    src = T.xs[:, j * TC:(j + 1) * TC]
+                    dst = T.rs[:, k * TC:(k + 1) * TC]
+                m = mine[cores[j]]
+                trs.append(RemoteDMATransfer(dst_ids=[DstId(rid=rid, pnc=pid)], dma_engine_mask=m,
+                                             remote_sem=S["arr%d" % k], src=src, dst=dst))
+                left += m.bit_count()
+            g.remote_dma_fused(trs, local_sem=S.sent)
+
+    same_die = [j for j in far if topo.die(cores[j]) == topo.die(core)]
+    order = [r] + near + same_die + [j for j in far if j not in same_die]
+    g.tensor.wait_ge(S.qxo, 1)
+    g.tensor.wait_ge(S.qwn, len(_runs(near + [r])))
+    waited_far = False
+    for i, j in enumerate(order):
+        if j == r:
+            rhs, rsc = T.xq[:, r * TC:(r + 1) * TC], T.xs[:, r * TC:(r + 1) * TC]
+        else:
+            k = _slot(r, j)
+            rhs, rsc = T.rq[:, k * TC:(k + 1) * TC], T.rs[:, k * TC:(k + 1) * TC]
+            if j in far and not waited_far:
+                g.tensor.wait_ge(S.qwf, len(_runs(far)))
+                waited_far = True
+            g.tensor.wait_ge(S["arr%d" % k], 2 * _masks(topo, cores, cores[j])[core].bit_count())
+        mmi = g.tensor.matmul_mx(T.acc[:, 0:TC], T.wq[:, j * TC:(j + 1) * TC], T.ws[:, j * TC:(j + 1) * TC],
+                                 rhs, rsc, i == 0, i == N - 1)
+    mmi.then_inc(S.mm, 1)
+
+    g.vector.wait_ge(S.mm, 1)
+    g.vector.tensor_copy(T.yb[:], T.acc[:, 0:TC]).then_inc(S.cp, 1)
+    g.sync.wait_ge(S.cp, 1)
+    g.sync.dma_start(T.y[:], T.yb[:]).then_inc(S.st, 16)
+    g.sync.wait_ge(S.st, 16)
+    g.wait_ge(S.sent, left)

@@ -17,8 +17,8 @@ SCRATCH = {
     "acc": ("psum", [128, 512], "float32"),
     "yb": ("sbuf", [128, TC], "float32"),
 }
-SEMAPHORES = ["lxf", "lxn", "lxo", "lwn", "lwf", "qxf", "qxn", "qxo", "qwn", "qwf",
-              "sent", "mm", "cp", "st"] + ["arr%d" % k for k in range(N - 1)]
+SEMAPHORES = (["lx%d" % j for j in range(N)] + ["qx%d" % j for j in range(N)] + ["lwn", "lwf", "qwn", "qwf",
+              "sent", "mm", "cp", "st"] + ["arr%d" % k for k in range(N - 1)])
 
 
 def _one_chip(topo, a, b):
@@ -35,29 +35,26 @@ def _runs(ranks):
     return out
 
 
-def _share(engines, parts):
-    per = 1
-    while per * 2 * parts <= len(engines):
-        per *= 2
-    return [sum(1 << e for e in engines[k * per:(k + 1) * per]) for k in range(parts)]
+def _pow2(engines):
+    n = 1
+    while n * 2 <= len(engines):
+        n *= 2
+    return sum(1 << e for e in engines[:n])
 
 
-def _masks(topo, cores, src):
-    far = [c for c in cores if c != src and not _one_chip(topo, c, src)]
-    near = [c for c in cores if c != src and _one_chip(topo, c, src)]
-    out, used = {}, 0
-    for group in (far, near):
-        if not group:
-            continue
-        can = topo.mask(src, group[0])
-        for c in group:
-            can &= topo.mask(src, c)
-        engines = [e for e in range(can.bit_length()) if can >> e & 1]
-        free = [e for e in engines if not used >> e & 1]
-        for c, m in zip(group, _share(free if len(free) >= len(group) else engines, len(group))):
-            out[c] = m
-            used |= m
-    return out
+def _plan(topo, cores, src):
+    far = [j for j, c in enumerate(cores) if not _one_chip(topo, c, src)]
+    far.sort(key=lambda j: topo.die(cores[j]) == topo.die(src))
+    near = [j for j, c in enumerate(cores) if c != src and _one_chip(topo, c, src)]
+    masks, out = {}, 0
+    for j in far:
+        m = topo.mask(src, cores[j])
+        masks[j] = _pow2([e for e in range(m.bit_length()) if m >> e & 1])
+        out |= masks[j]
+    for j in near:
+        m = topo.mask(src, cores[j])
+        masks[j] = _pow2([e for e in range(m.bit_length()) if m >> e & 1 and not out >> e & 1])
+    return far, near, masks
 
 
 def _slot(r, j):
@@ -69,8 +66,7 @@ def rank_program(g, core, T, topo):
     if r is None:
         return
     cores, S = T.cores, T.sem
-    far = [j for j in range(N) if not _one_chip(topo, cores[j], core)]
-    near = [j for j in range(N) if j != r and _one_chip(topo, cores[j], core)]
+    far, near, masks = _plan(topo, cores, core)
 
     def load(q, buf, src, ranks, sem):
         for a, n in _runs(ranks):
@@ -82,27 +78,26 @@ def rank_program(g, core, T, topo):
             g.vector.quantize_mx(codes[:, a * TC:(a + n) * TC], plane[:, a * TC:(a + n) * TC],
                                  buf[:, a * TB:(a + n) * TB]).then_inc(qsem, 1)
 
-    load(g.sync, T.xb, T.x, far, S.lxf)
-    load(g.scalar, T.xb, T.x, near, S.lxn)
-    load(g.scalar, T.xb, T.x, [r], S.lxo)
+    for j in far:
+        load(g.sync, T.xb, T.x, [j], S["lx%d" % j])
+    for j in near + [r]:
+        load(g.scalar, T.xb, T.x, [j], S["lx%d" % j])
     load(g.sync, T.wb, T.w, near + [r], S.lwn)
     load(g.scalar, T.wb, T.w, far, S.lwf)
 
-    quant(T.xq, T.xs, T.xb, far, S.lxf, S.qxf)
-    quant(T.xq, T.xs, T.xb, near, S.lxn, S.qxn)
-    quant(T.xq, T.xs, T.xb, [r], S.lxo, S.qxo)
+    for j in far + near + [r]:
+        quant(T.xq, T.xs, T.xb, [j], S["lx%d" % j], S["qx%d" % j])
     quant(T.wq, T.ws, T.wb, near + [r], S.lwn, S.qwn)
     quant(T.wq, T.ws, T.wb, far, S.lwf, S.qwf)
 
-    mine = _masks(topo, cores, core)
+    stages = [[j] for j in far[:-1]] + [far[-1:] + near]
     left = 0
-    for group, qsem in ((far, S.qxf), (near, S.qxn)):
-        if not group:
-            continue
-        g.wait_ge(qsem, len(_runs(group)))
+    for stage in stages:
+        for j in stage:
+            g.wait_ge(S["qx%d" % j], 1)
         for what in ("codes", "plane"):
             trs = []
-            for j in group:
+            for j in stage:
                 rid, pid = topo.addr(cores[j], core)
                 k = _slot(j, r)
                 if what == "codes":
@@ -111,15 +106,16 @@ def rank_program(g, core, T, topo):
                 else:
                     src = T.xs[:, j * TC:(j + 1) * TC]
                     dst = T.rs[:, k * TC:(k + 1) * TC]
-                m = mine[cores[j]]
-                trs.append(RemoteDMATransfer(dst_ids=[DstId(rid=rid, pnc=pid)], dma_engine_mask=m,
+                trs.append(RemoteDMATransfer(dst_ids=[DstId(rid=rid, pnc=pid)], dma_engine_mask=masks[j],
                                              remote_sem=S["arr%d" % k], src=src, dst=dst))
-                left += m.bit_count()
+                left += masks[j].bit_count()
             g.remote_dma_fused(trs, local_sem=S.sent)
 
-    same_die = [j for j in far if topo.die(cores[j]) == topo.die(core)]
-    order = [r] + near + same_die + [j for j in far if j not in same_die]
-    g.tensor.wait_ge(S.qxo, 1)
+    def stage_of(j):
+        f = _plan(topo, cores, cores[j])[0]
+        return (f.index(r), 1) if r in f else (len(f) - 1, 0)
+    order = [r] + sorted(near + far, key=stage_of)
+    g.tensor.wait_ge(S["qx%d" % r], 1)
     g.tensor.wait_ge(S.qwn, len(_runs(near + [r])))
     waited_far = False
     for i, j in enumerate(order):
@@ -131,7 +127,7 @@ def rank_program(g, core, T, topo):
             if j in far and not waited_far:
                 g.tensor.wait_ge(S.qwf, len(_runs(far)))
                 waited_far = True
-            g.tensor.wait_ge(S["arr%d" % k], 2 * _masks(topo, cores, cores[j])[core].bit_count())
+            g.tensor.wait_ge(S["arr%d" % k], 2 * _plan(topo, cores, cores[j])[2][r].bit_count())
         mmi = g.tensor.matmul_mx(T.acc[:, 0:TC], T.wq[:, j * TC:(j + 1) * TC], T.ws[:, j * TC:(j + 1) * TC],
                                  rhs, rsc, i == 0, i == N - 1)
     mmi.then_inc(S.mm, 1)

from concourse.bass import DstId, RemoteDMATransfer
from concourse.mybir import dt

N = 4
TB = 512
TC = 128

SCRATCH = {
    "xb": ("sbuf", [128, N * TB], "bfloat16"),
    "wb": ("sbuf", [128, N * TB], "bfloat16"),
    "xq": ("sbuf", [128, N * TC], "float8_e4m3fn_x4"),
    "xs": ("sbuf", [128, N * TC], "uint8"),
    "wq": ("sbuf", [128, N * TC], "float8_e4m3fn_x4"),
    "ws": ("sbuf", [128, N * TC], "uint8"),
    "rq": ("sbuf", [128, (N - 1) * TC], "float8_e4m3fn_x4"),
    "rs": ("sbuf", [128, (N - 1) * TC], "uint8"),
    "acc": ("psum", [128, 512], "float32"),
    "yb": ("sbuf", [128, TC], "float32"),
}
SEMAPHORES = (["lx%d" % j for j in range(N)] + ["qx%d" % j for j in range(N)] + ["lwn", "lwf", "qwn", "qwf",
              "sent", "mm", "cp", "st"] + ["arr%d" % k for k in range(N - 1)])


def _one_chip(topo, a, b):
    return topo.host(a) == topo.host(b) and topo.chip(a) == topo.chip(b)


def _runs(ranks):
    out = []
    for j in sorted(ranks):
        if out and out[-1][0] + out[-1][1] == j:
            out[-1][1] += 1
        else:
            out.append([j, 1])
    return out


def _pow2(engines):
    n = 1
    while n * 2 <= len(engines):
        n *= 2
    return sum(1 << e for e in engines[:n])


def _plan(topo, cores, src):
    far = [j for j, c in enumerate(cores) if not _one_chip(topo, c, src)]
    far.sort(key=lambda j: topo.die(cores[j]) == topo.die(src))
    near = [j for j, c in enumerate(cores) if c != src and _one_chip(topo, c, src)]
    masks, out = {}, 0
    for j in far:
        m = topo.mask(src, cores[j])
        masks[j] = _pow2([e for e in range(m.bit_length()) if m >> e & 1])
        out |= masks[j]
    for j in near:
        m = topo.mask(src, cores[j])
        masks[j] = _pow2([e for e in range(m.bit_length()) if m >> e & 1 and not out >> e & 1])
    return far, near, masks


def _slot(r, j):
    return j if j < r else j - 1


def rank_program(g, core, T, topo):
    r = T.rank_of(core)
    if r is None:
        return
    cores, S = T.cores, T.sem
    far, near, masks = _plan(topo, cores, core)

    def load(q, buf, src, ranks, sem):
        for a, n in _runs(ranks):
            q.dma_start(buf[:, a * TB:(a + n) * TB], src[:, a * TB:(a + n) * TB]).then_inc(sem, 16)

    def quant(codes, plane, buf, ranks, lsem, qsem):
        g.vector.wait_ge(lsem, 16 * len(_runs(ranks)))
        for a, n in _runs(ranks):
            g.vector.quantize_mx(codes[:, a * TC:(a + n) * TC], plane[:, a * TC:(a + n) * TC],
                                 buf[:, a * TB:(a + n) * TB]).then_inc(qsem, 1)

    for j in far:
        load(g.sync, T.xb, T.x, [j], S["lx%d" % j])
    for j in near + [r]:
        load(g.scalar, T.xb, T.x, [j], S["lx%d" % j])
    load(g.sync, T.wb, T.w, near + [r], S.lwn)
    load(g.scalar, T.wb, T.w, far, S.lwf)

    for j in far + near + [r]:
        quant(T.xq, T.xs, T.xb, [j], S["lx%d" % j], S["qx%d" % j])
    quant(T.wq, T.ws, T.wb, near + [r], S.lwn, S.qwn)
    quant(T.wq, T.ws, T.wb, far, S.lwf, S.qwf)

    stages = [[j] for j in far[:-1]] + [far[-1:] + near]
    left = 0
    for stage in stages:
        for j in stage:
            g.wait_ge(S["qx%d" % j], 1)
        for what in ("codes", "plane"):
            trs = []
            for j in stage:
                rid, pid = topo.addr(cores[j], core)
                k = _slot(j, r)
                if what == "codes":
                    src = T.xq[:, j * TC:(j + 1) * TC].bitcast(dt.uint8)
                    dst = T.rq[:, k * TC:(k + 1) * TC].bitcast(dt.uint8)
                else:
                    src = T.xs[:, j * TC:(j + 1) * TC]
                    dst = T.rs[:, k * TC:(k + 1) * TC]
                trs.append(RemoteDMATransfer(dst_ids=[DstId(rid=rid, pnc=pid)], dma_engine_mask=masks[j],
                                             remote_sem=S["arr%d" % k], src=src, dst=dst))
                left += masks[j].bit_count()
            g.remote_dma_fused(trs, local_sem=S.sent)

    def stage_of(j):
        f = _plan(topo, cores, cores[j])[0]
        return (f.index(r), 1) if r in f else (len(f) - 1, 0)
    order = [r] + sorted(near + far, key=stage_of)
    g.tensor.wait_ge(S["qx%d" % r], 1)
    g.tensor.wait_ge(S.qwn, len(_runs(near + [r])))
    waited_far = False
    for i, j in enumerate(order):
        if j == r:
            rhs, rsc = T.xq[:, r * TC:(r + 1) * TC], T.xs[:, r * TC:(r + 1) * TC]
        else:
            k = _slot(r, j)
            rhs, rsc = T.rq[:, k * TC:(k + 1) * TC], T.rs[:, k * TC:(k + 1) * TC]
            if j in far and not waited_far:
                g.tensor.wait_ge(S.qwf, len(_runs(far)))
                waited_far = True
            g.tensor.wait_ge(S["arr%d" % k], 2 * _plan(topo, cores, cores[j])[2][r].bit_count())
        mmi = g.tensor.matmul_mx(T.acc[:, 0:TC], T.wq[:, j * TC:(j + 1) * TC], T.ws[:, j * TC:(j + 1) * TC],
                                 rhs, rsc, i == 0, i == N - 1)
    mmi.then_inc(S.mm, 1)

    g.vector.wait_ge(S.mm, 1)
    g.vector.tensor_copy(T.yb[:], T.acc[:, 0:TC]).then_inc(S.cp, 1)
    g.sync.wait_ge(S.cp, 1)
    g.sync.dma_start(T.y[:], T.yb[:]).then_inc(S.st, 16)
    g.sync.wait_ge(S.st, 16)
    g.wait_ge(S.sent, left)
